import numpy as np
import ml_dtypes


def mxq(x, axis, fmt="e4m3"):
    dtype, down = {"e4m3": (ml_dtypes.float8_e4m3fn, 7), "e5m2": (ml_dtypes.float8_e5m2, 14)}[fmt]
    v = np.moveaxis(np.asarray(x, np.float32).astype(ml_dtypes.bfloat16).astype(np.float64), axis, -1)
    blocks = v.reshape(v.shape[:-1] + (-1, 32))
    amax = np.abs(blocks).max(-1, keepdims=True)
    byte = np.maximum(np.where(amax > 0, np.frexp(amax)[1] - 1 + 127, 0) - down, 1)
    scale = np.exp2(byte - 127.0)
    codes = (blocks / scale).astype(np.float32).astype(dtype).astype(np.float64)
    return np.moveaxis((codes * scale).reshape(v.shape), -1, axis)


WIDE = False


def mx_kscale(k):
    if not WIDE:
        return np.ones(k)
    levels = np.array([10, -10, 5, -5, 0])
    if k % 512:
        return np.exp2(np.random.permutation(np.resize(levels, k // 32))).repeat(32)
    a = np.empty((k // 512, 16))
    for p in range(k // 512):
        a[p, :8] = np.random.permutation(np.resize(levels, 8))
        for g in range(8):
            far = levels[np.abs(levels - a[p, g]) >= 10]
            a[p, g + 8] = far[np.random.randint(len(far))]
    return np.exp2(a.ravel()).repeat(32)


BF16 = ml_dtypes.bfloat16


def bf(x):
    return np.asarray(x, np.float32).astype(BF16)


def f64(x):
    return np.asarray(x).astype(np.float64)


E2M1 = np.array([0.0, 0.5, 1.0, 1.5, 2.0, 3.0, 4.0, 6.0, -0.0, -0.5, -1.0, -1.5, -2.0, -3.0, -4.0, -6.0])


def pack_weight(w, fmt):
    k, n = w.shape
    w = f64(bf(w)).reshape(k // 32, 32, n)
    amax = np.abs(w).max(1)
    if fmt == "e4m3":
        byte = np.frexp(amax)[1] - 1 + 127 - 7
    else:
        mant, ex = np.frexp(amax / 6.0)
        byte = np.where(mant > 0.5, ex, ex - 1) + 127
    byte = np.clip(np.where(amax > 0, byte, 1), 1, 254)
    scaled = (w * np.exp2(127.0 - byte)[:, None, :]).reshape(k, n).astype(np.float32)
    by_word = np.ascontiguousarray(scaled.reshape(k // 512, 128, 4, n).transpose(0, 1, 3, 2))
    if fmt == "e4m3":
        words = by_word.astype(ml_dtypes.float8_e4m3fn).view(np.uint8)
    else:
        c = by_word.astype(ml_dtypes.float4_e2m1fn).view(np.uint8) & 0xF
        words = c[..., 0::2] | (c[..., 1::2] << 4)
    return np.ascontiguousarray(words), np.ascontiguousarray(byte.astype(np.uint8).reshape(k // 512, 16, n))


def unpack_weight(words, scales, fmt):
    g, p, n, _ = words.shape
    if fmt == "e4m3":
        vals = np.ascontiguousarray(words).view(ml_dtypes.float8_e4m3fn).astype(np.float64)
    else:
        nib = np.empty((g, p, n, 4), np.uint8)
        nib[..., 0::2] = words & 0xF
        nib[..., 1::2] = words >> 4
        vals = E2M1[nib]
    vals = vals * np.repeat(np.exp2(scales.astype(np.float64) - 127.0), 8, axis=1)[..., None]
    return vals.transpose(0, 1, 3, 2).reshape(g * 512, n)
def pack4(w):
    words, scales = pack_weight(w, "e2m1")
    return words.reshape(words.shape[0], 128, -1), scales


def unpack4(words, scales):
    return unpack_weight(words.reshape(words.shape[0], 128, -1, 2), scales, "e2m1")


M, F, N = 2048, 1024, 512


def setup_inputs():
    r = mx_kscale(M)
    x = np.random.standard_normal((M, F)) * r[:, None]
    prob = 1.0 / (1.0 + np.exp(-1.5 * np.random.standard_normal(M)))
    c = 4.0 * np.random.standard_normal((M, N)) / np.sqrt(M) / r[:, None]
    d = 4.0 * np.random.standard_normal((M, N)) / np.sqrt(M) / r[:, None]
    e = 4.0 * np.random.standard_normal((M, N)) / np.sqrt(M) / r[:, None]
    c_words, c_scales = pack4(c)
    d_words, d_scales = pack_weight(d, "e4m3")
    return {"x": bf(x),
            "prob": bf(prob),
            "c_words": c_words, "c_scales": c_scales,
            "d_words": d_words, "d_scales": d_scales,
            "e": bf(e),
            "alpha": bf(0.7 + 0.2 * np.random.standard_normal(N))}


def reference(x, prob, c_words, c_scales, d_words, d_scales, e, alpha):
    pr = f64(prob)
    v = pr * (1.0 - pr)
    a = mxq(f64(x) * v[:, None], 0, "e4m3")
    hc = a.T @ unpack4(c_words, c_scales)
    hd = a.T @ unpack_weight(d_words, d_scales, "e4m3")
    he = a.T @ mxq(f64(e), 0, "e4m3")
    return hc + f64(alpha) * hd + he

@@ -1,0 +1,265 @@
+from contextlib import ExitStack
+
+import concourse.mybir as mybir
+from concourse.masks import make_identity
+
+M, F, N = 2048, 1024, 512
+FLOPS = 3 * 2 * M * F * N
+
+F32 = mybir.dt.float32
+BF16 = mybir.dt.bfloat16
+I32 = mybir.dt.int32
+U32 = mybir.dt.uint32
+U8 = mybir.dt.uint8
+FP8X4 = mybir.dt.float8_e4m3fn_x4
+FP4X4 = mybir.dt.float4_e2m1fn_x4
+ALU = mybir.AluOpType
+
+P = 128
+PACK = 4
+G = 4
+
+LOADS = ["prob","x0a","x0b","ds0","ds1","ds2","ds3","x1","d0","cs0","cs1","cs2","cs3","c0","x2","d1","c1","x3","e0","d2","c2","e1","d3","e2","c3","e3","y0","y1","y2","y3"]
+V_ORDER = ["nv","SAx0a","SAx0b","IA011","IA001","QA001","QA011","SAx1","QA021","IA131","IA111","IA121","QA031","QA102","SAx2","QA122","IA211","IA231","SAx3","QA222","IA301","IA321","QA202","IA331","IE002","QA322","QA302","IE102","QE004","IE202","P11","P10","QE104","QE204","SAy0","QE304","SAy1","QA042","P20","P21","SAy2","QA142","SAy3","QA242","IA342","IA062","QA342","P12","QA262","QA062","QA162","P22","QA362","P14","P13","P15","P23","P25","P24","P16","P17","P26","P27"]
+S_ORDER = ["alpha","IA021","IA031","IA101","IA201","IA221","IE022","IA311","IE122","IE222","IE302","IE322","IA042","IA142","IA242","IA262","IA162","IA362"]
+PE_ORDER = ["D00","D01","D02","D03","C00","C01","C02","C03","D10","D11","D12","D13","C10","C11","C12","C13","D20","D21","D22","D23","C20","C21","C22","C23","D30","D31","D32","D33","C30","C31","C32","C33","E00","E01","E02","E03","E10","E11","E12","E13","E20","E21","E22","E23","E30","E31","E32","E33","D04","D05","E04","E05","C04","C05","D14","D15","E14","E15","C14","C15","D24","D25","E24","E25","C24","C25","D34","D35","E34","E35","C34","C35","D06","D16","D26","D36","C06","C16","C26","C36","E06","E16","E26","E36","D07","D17","D27","D37","C07","C17","C27","C37","E07","E17","E27","E37"]
+X_PIECES = [["x0a",0,0,256],["x0b",0,256,256],["x1",1,0,512],["x2",2,0,512],["x3",3,0,512],["y0",0,512,512],["y1",1,512,512],["y2",2,512,512],["y3",3,512,512]]
+
+
+def tile_logistic_hessian_block_s10_kernel(
+    tc, x, prob, c_words, c_scales, d_words, d_scales, e, alpha, out
+):
+    nc = tc.nc
+    with ExitStack() as ctx:
+        sb = ctx.enter_context(tc.tile_pool(name="sb", bufs=1))
+        ps = ctx.enter_context(tc.psum_pool(name="ps", bufs=1))
+        ctx.enter_context(tc.manual_schedule())
+
+        prob_t = sb.tile([P, G, 16], BF16, name="prob_t")
+        negv = sb.tile([P, G, PACK], F32, name="negv")
+        alpha_t = sb.tile([P, PACK], BF16, name="alpha_t")
+        alpha_all = sb.tile([P, N], F32, name="alpha_all")
+        ident = sb.tile([P, P], BF16, name="ident")
+        warm = sb.tile([P, 2], BF16, name="warm")
+        warm2 = sb.tile([P, 2], BF16, name="warm2")
+        c_plane = sb.tile([P, G, N], U8, name="c_plane", align_bytes=64)
+        d_plane = sb.tile([P, N], U8, name="d_plane", align_bytes=64)
+        c_t = [sb.tile([P, 2 * N], U8, name="c_t%d" % g, align_bytes=64) for g in range(G)]
+        d_t = [sb.tile([P, N], U32, name="d_t%d" % g, align_bytes=64) for g in range(G)]
+        e_raw = [sb.tile([P, PACK, N], BF16, name="e_raw%d" % g, align_bytes=64) for g in range(G)]
+        e_codes = [sb.tile([P, N], U32, name="e_codes%d" % g, align_bytes=64) for g in range(G)]
+        e_plane = [sb.tile([P, N], U8, name="e_plane%d" % g, align_bytes=64) for g in range(G)]
+        x_raw = {}
+        a_rows = {}
+        for nm, g, c0, w in X_PIECES:
+            x_raw[nm] = sb.tile([P, PACK, w], BF16, name="xr_" + nm, align_bytes=64)
+            a_rows[nm] = sb.tile([P, PACK, w], BF16, name="ar_" + nm, align_bytes=64)
+        pieces = {nm: (g, c0, w) for nm, g, c0, w in X_PIECES}
+        grouped = {}
+        a_codes = {}
+        banks = {}
+        scaled = {}
+        result = {}
+        done = set()
+
+        def load(nm):
+            if nm == "prob":
+                nc.sync.dma_start(out=prob_t[:, :, 0:PACK], in_=prob.rearrange("(g p j) -> p g j", p=P, j=PACK))
+            elif nm[0] in "xy":
+                g, c0, w = pieces[nm]
+                src = x[512 * g : 512 * (g + 1), c0 : c0 + w].rearrange("(p j) w -> p j w", j=PACK)
+                nc.sync.dma_start(out=x_raw[nm][:], in_=src)
+            elif nm[0] == "e":
+                g = int(nm[1])
+                src = e[512 * g : 512 * (g + 1), :].rearrange("(p j) w -> p j w", j=PACK)
+                nc.sync.dma_start(out=e_raw[g][:], in_=src)
+            elif nm[:2] == "ds":
+                q = int(nm[2])
+                nc.sync.dma_start(
+                    out=d_plane[32 * q : 32 * q + 16, :].bitcast(I32),
+                    in_=d_scales[:, 4 * q : 4 * q + 4, :].bitcast(I32),
+                )
+            elif nm[:2] == "cs":
+                q = int(nm[2])
+                nc.sync.dma_start(
+                    out=c_plane[32 * q : 32 * q + 4, :, :].bitcast(I32),
+                    in_=c_scales[:, 4 * q : 4 * q + 4, :].rearrange("g r n -> r g n").bitcast(I32),
+                )
+            elif nm[0] == "d":
+                g = int(nm[1])
+                nc.sync.dma_start(
+                    out=d_t[g][:].bitcast(I32),
+                    in_=d_words[g].rearrange("p n t -> p (n t)").bitcast(I32),
+                )
+            else:
+                g = int(nm[1])
+                nc.sync.dma_start(out=c_t[g][:].bitcast(I32), in_=c_words[g].bitcast(I32))
+            done.add(nm)
+
+        def interleave(on_vector, dst, src):
+            o = dst.rearrange("p (c i) t -> p c t i", i=4)
+            s = src.rearrange("p t (c i) -> p c t i", i=4)
+            if on_vector:
+                nc.vector.tensor_copy(out=o, in_=s)
+            else:
+                nc.scalar.copy(out=o, in_=s)
+
+        def piece_of(g, c0):
+            for nm, pg, p0, w in X_PIECES:
+                if pg == g and p0 <= c0 < p0 + w:
+                    return nm, c0 - p0
+            raise ValueError(c0)
+
+        def last_of(t, kinds):
+            return [s for s in PE_ORDER if s[0] in kinds and int(s[2]) == t][-1]
+
+        def first_of(t, kinds):
+            return [s for s in PE_ORDER if s[0] in kinds and int(s[2]) == t][0]
+
+        def quant_step(kind, g, t):
+            for s in V_ORDER:
+                if s[:2] == "Q" + kind and int(s[2]) == g and int(s[3]) <= t < int(s[3]) + int(s[4]):
+                    return s
+            raise ValueError(t)
+
+        def needs(s):
+            k = s[:2]
+            if s == "nv":
+                return ["prob"]
+            if s == "alpha":
+                return []
+            if k == "SA":
+                return ["nv", s[2:]]
+            if k == "IA":
+                return ["SA" + piece_of(int(s[2]), 128 * int(s[3]))[0]]
+            if k == "IE":
+                return ["e" + s[2]]
+            if k in ("QA", "QE"):
+                g, t0, nt = int(s[2]), int(s[3]), int(s[4])
+                return [
+                    u for u in V_ORDER + S_ORDER
+                    if u[:2] == "I" + k[1] and int(u[2]) == g and t0 <= int(u[3]) < t0 + nt
+                ]
+            if k == "P1":
+                return [last_of(int(s[2]), "D"), "alpha"]
+            if k == "P2":
+                return [last_of(int(s[2]), "CE"), "P1" + s[2]]
+            g, t = int(s[1]), int(s[2])
+            d = [quant_step("A", g, t)]
+            if s[0] == "D":
+                d += ["d%d" % g, "ds3"] + (["P1%d" % (t - 4)] if t >= 4 else [])
+            else:
+                d += ["P2%d" % (t - 4)] if t >= 4 else ["alpha"]
+            if s[0] == "C":
+                d += ["c%d" % g, "cs3"]
+            if s[0] == "E":
+                d += [quant_step("E", g, u) for u in range(4)]
+            return d
+
+        def group_tile(kind, g, t):
+            q = quant_step(kind, g, t)
+            if q not in grouped:
+                grouped[q] = sb.tile([P, 128 * int(q[4]), PACK], BF16, name="gr_" + q, align_bytes=64)
+            return grouped[q], 128 * (t - int(q[3]))
+
+        def step(s, on_vector):
+            k = s[:2]
+            if s == "nv":
+                nc.vector.scalar_tensor_tensor(
+                    out=negv[:], in0=prob_t[:, :, 0:PACK], scalar=1.0, in1=prob_t[:, :, 0:PACK],
+                    op0=ALU.subtract, op1=ALU.mult,
+                )
+            elif s == "alpha":
+                spread = ps.tile([P, PACK, P], BF16, name="spread", tag="bank7")
+                for m in range(PACK):
+                    nc.tensor.transpose(spread[:, m, :], alpha_t[:, m : m + 1].to_broadcast([P, P]), ident[:])
+                nc.scalar.copy(
+                    out=alpha_all[:].rearrange("q (p m) -> q p m", m=PACK),
+                    in_=spread[:].rearrange("q m p -> q p m"),
+                )
+            elif k == "SA":
+                nm = s[2:]
+                g = pieces[nm][0]
+                for j in range(PACK):
+                    nc.vector.tensor_scalar(
+                        out=a_rows[nm][:, j, :], in0=x_raw[nm][:, j, :], scalar1=negv[:, g, j : j + 1],
+                        scalar2=-1.0, op0=ALU.mult, op1=ALU.mult,
+                    )
+            elif k in ("IA", "IE"):
+                g, t0, nt = int(s[2]), int(s[3]), int(s[4])
+                dst, o0 = group_tile(k[1], g, t0)
+                if k == "IA":
+                    nm, c0 = piece_of(g, 128 * t0)
+                    src = a_rows[nm][:, :, c0 : c0 + 128 * nt]
+                else:
+                    src = e_raw[g][:, :, 128 * t0 : 128 * (t0 + nt)]
+                interleave(on_vector, dst[:, o0 : o0 + 128 * nt, :], src)
+            elif k == "QA":
+                g, t0, nt = int(s[2]), int(s[3]), int(s[4])
+                codes = sb.tile([P, 128 * nt], U32, name="ac_" + s, align_bytes=64)
+                plane = sb.tile([P, 128 * nt], U8, name="ap_" + s, align_bytes=64)
+                nc.vector.quantize_mx(
+                    out=codes[:].bitcast(FP8X4), scales=plane[:],
+                    in_=grouped[s][:].rearrange("p w j -> p (w j)"),
+                )
+                for u in range(nt):
+                    a_codes[(g, t0 + u)] = (codes[:, 128 * u : 128 * (u + 1)], plane[:, 128 * u : 128 * (u + 1)])
+            elif k == "QE":
+                g, t0, nt = int(s[2]), int(s[3]), int(s[4])
+                cols = slice(128 * t0, 128 * (t0 + nt))
+                nc.vector.quantize_mx(
+                    out=e_codes[g][:, cols].bitcast(FP8X4), scales=e_plane[g][:, cols],
+                    in_=grouped[s][:].rearrange("p w j -> p (w j)"),
+                )
+            elif k == "P1":
+                t = int(s[2])
+                scaled[t] = sb.tile([P, N], F32, name="scaled%d" % t)
+                nc.vector.tensor_tensor(out=scaled[t][:], in0=banks[("D", t)][:], in1=alpha_all[:], op=ALU.mult)
+            elif k == "P2":
+                t = int(s[2])
+                result[t] = sb.tile([P, N], F32, name="result%d" % t)
+                parts = 2 if t == 7 else 1
+                w = N // parts
+                for h in range(parts):
+                    cols = slice(h * w, (h + 1) * w)
+                    nc.vector.tensor_tensor(
+                        out=result[t][:, cols], in0=banks[("P", t)][:, cols], in1=scaled[t][:, cols], op=ALU.add
+                    )
+                    nc.sync.dma_start(out=out[128 * t : 128 * (t + 1), cols], in_=result[t][:, cols])
+            else:
+                g, t = int(s[1]), int(s[2])
+                kinds = "D" if s[0] == "D" else "CE"
+                key = ("D" if s[0] == "D" else "P", t)
+                if key not in banks:
+                    b = t % 4 + (0 if s[0] == "D" else 4)
+                    banks[key] = ps.tile([P, N], F32, name="acc%s%d" % key, tag="bank%d" % b)
+                codes, plane = a_codes[(g, t)]
+                if s[0] == "D":
+                    rhs, rs = d_t[g][:].bitcast(FP8X4), d_plane[4 * g :, :]
+                elif s[0] == "C":
+                    rhs, rs = c_t[g][:].bitcast(FP4X4), c_plane[:, g, :]
+                else:
+                    rhs, rs = e_codes[g][:].bitcast(FP8X4), e_plane[g][:]
+                nc.tensor.matmul_mx(
+                    out=banks[key][:], lhsT=codes.bitcast(FP8X4), lhsT_scale=plane, rhs=rhs, rhs_scale=rs,
+                    start=(s == first_of(t, kinds)), stop=(s == last_of(t, kinds)),
+                )
+            done.add(s)
+
+        nc.gpsimd.dma_start(out=alpha_t[:], in_=alpha.rearrange("(p m) -> p m", m=PACK))
+        make_identity(nc, ident[:])
+        nc.vector.memset(d_plane[:].bitcast(I32), 0)
+        nc.vector.memset(c_plane[:].rearrange("p g n -> p (g n)").bitcast(I32), 0)
+        nc.vector.memset(warm[:], 0.0)
+        nc.scalar.copy(out=warm2[:], in_=warm[:])
+        for nm in LOADS:
+            load(nm)
+        queues = [(list(V_ORDER), True), (list(S_ORDER), False), (list(PE_ORDER), False)]
+        while any(q for q, v in queues):
+            moved = False
+            for q, v in queues:
+                while q and all(d in done for d in needs(q[0])):
+                    step(q[0], v)
+                    q.remove(q[0])
+                    moved = True
+            assert moved

@@ -16,250 +16,315 @@ FP4X4 = mybir.dt.float4_e2m1fn_x4
 ALU = mybir.AluOpType
 
 P = 128
-PACK = 4
-G = 4
+SLOTS = 4
+K_PASS = P * SLOTS
+GROUPS = M // K_PASS
+TILES = F // P
+OPEN_TILES = 4
+LAST = TILES - 1
+HALF = N // 2
+QUADRANTS = 4
+ALIGN = 256
+TURNED_COLUMNS = 8
+IDLE_PASSES = (10, 3, 10)
 
-LOADS = ["prob","x0a","x0b","ds0","ds1","ds2","ds3","x1","d0","cs0","cs1","cs2","cs3","c0","x2","d1","c1","x3","e0","d2","c2","e1","d3","e2","c3","e3","y0","y1","y2","y3"]
-V_ORDER = ["nv","SAx0a","SAx0b","IA011","IA001","QA001","QA011","SAx1","QA021","IA131","IA111","IA121","QA031","QA102","SAx2","QA122","IA211","IA231","SAx3","QA222","IA301","IA321","QA202","IA331","IE002","QA322","QA302","IE102","QE004","IE202","P11","P10","QE104","QE204","SAy0","QE304","SAy1","QA042","P20","P21","SAy2","QA142","SAy3","QA242","IA342","IA062","QA342","P12","QA262","QA062","QA162","P22","QA362","P14","P13","P15","P23","P25","P24","P16","P17","P26","P27"]
-S_ORDER = ["alpha","IA021","IA031","IA101","IA201","IA221","IE022","IA311","IE122","IE222","IE302","IE322","IA042","IA142","IA242","IA262","IA162","IA362"]
-PE_ORDER = ["D00","D01","D02","D03","C00","C01","C02","C03","D10","D11","D12","D13","C10","C11","C12","C13","D20","D21","D22","D23","C20","C21","C22","C23","D30","D31","D32","D33","C30","C31","C32","C33","E00","E01","E02","E03","E10","E11","E12","E13","E20","E21","E22","E23","E30","E31","E32","E33","D04","D05","E04","E05","C04","C05","D14","D15","E14","E15","C14","C15","D24","D25","E24","E25","C24","C25","D34","D35","E34","E35","C34","C35","D06","D16","D26","D36","C06","C16","C26","C36","E06","E16","E26","E36","D07","D17","D27","D37","C07","C17","C27","C37","E07","E17","E27","E37"]
-X_PIECES = [["x0a",0,0,256],["x0b",0,256,256],["x1",1,0,512],["x2",2,0,512],["x3",3,0,512],["y0",0,512,512],["y1",1,512,512],["y2",2,512,512],["y3",3,512,512]]
+LOAD_ORDER = [
+    "alpha", "prob", "x 0 0 4", "d_scales", "d 0", "e 0", "x 1 0 4", "c 0", "c_scales", "x 2 0 4", "e 1",
+    "d 1", "c 1", "x 3 0 4", "c 2", "d 2", "e 2", "e 3", "d 3", "x 0 4 2", "c 3", "x 1 4 4", "x 2 4 4",
+    "x 0 6 2", "x 3 4 4",
+]
+
+VECTOR_ORDER = [
+    "variance", "weigh 0 0 4", "lay A 0 0 1", "lay A 0 1 1", "quantise A 0 0 1", "quantise A 0 2 1",
+    "quantise A 0 1 1", "lay E 0 2 2", "quantise A 0 3 1", "weigh 1 0 4", "quantise E 0 0 4", "lay A 1 2 1",
+    "weigh 2 0 4", "quantise A 1 2 2", "quantise A 1 0 2", "lay E 1 2 2", "lay A 2 0 1", "quantise E 1 0 4",
+    "weigh 3 0 4", "quantise A 2 0 2", "lay A 3 2 1", "lay A 3 1 1", "quantise A 2 2 2", "lay E 2 2 2",
+    "quantise A 3 2 2", "quantise A 3 0 2", "lay E 3 2 2", "quantise E 2 0 4", "weigh 0 4 2", "scale 1",
+    "quantise E 3 0 4", "weigh 1 4 4", "scale 0", "quantise A 0 4 2", "add 0", "add 1", "weigh 2 4 4",
+    "quantise A 1 4 2", "weigh 0 6 2", "weigh 3 4 4", "quantise A 2 4 2", "lay A 3 4 2", "scale 2",
+    "quantise A 3 4 2", "lay A 1 6 2", "quantise A 0 6 2", "quantise A 1 6 2", "add 2", "quantise A 2 6 2",
+    "quantise A 3 6 2", "scale 5", "scale 3", "scale 4", "add 3", "scale 6", "add 4", "add 6", "add 5",
+    "scale 7", "add_c_last", "add_e_last 0", "add_e_last 1",
+]
+SCALAR_ORDER = [
+    "columns", "alpha", "lay A 0 2 1", "lay A 0 3 1", "lay E 0 0 2", "lay A 1 0 1", "lay A 1 3 1",
+    "lay A 1 1 1", "lay E 1 0 2", "lay A 2 1 1", "lay A 2 3 1", "lay A 2 2 1", "lay A 3 0 1", "lay A 3 3 1",
+    "lay E 2 0 2", "lay E 3 0 2", "lay A 0 5 1", "lay A 0 4 1", "lay A 1 4 2", "lay A 2 4 2", "lay A 0 6 2",
+    "lay A 2 6 2", "lay A 3 6 2",
+]
+FIRST_SWEEP = ["D0", "C0", "E0", "D1", "C1", "E1", "D2", "C2", "D3", "E2"]
+
+
+def tensor_order():
+    order = ["pass %s %s %d" % (b[0], b[1], t) for b in FIRST_SWEEP for t in range(OPEN_TILES)]
+    order += ["pass %s %d %d" % (w, GROUPS - 1, t) for t in range(OPEN_TILES) for w in "CE"]
+    for g in range(GROUPS):
+        order += ["pass %s %d %d" % (w, g, t) for w in ("DCE" if g == 0 else "DEC") for t in (4, 5)]
+    order += ["pass %s %d %d" % (w, g, LAST - 1) for w in "DCE" for g in range(GROUPS)]
+    order += ["pass %s %d %d" % (w, g, LAST) for w in "DC" for g in range(GROUPS)]
+    order += ["half_pass %d %d" % (h, g) for h in range(2) for g in range(GROUPS)]
+    return order
+
+
+def parse(step):
+    return tuple(w if w[0] not in "0123456789" else int(w) for w in step.split())
 
 
 def tile_logistic_hessian_block_s10_kernel(
     tc, x, prob, c_words, c_scales, d_words, d_scales, e, alpha, out
 ):
     nc = tc.nc
+    loads = [parse(s) for s in LOAD_ORDER]
+    on_vector = [parse(s) for s in VECTOR_ORDER]
+    on_scalar = [parse(s) for s in SCALAR_ORDER]
+    on_tensor = [parse(s) for s in tensor_order()]
+    x_parts = sorted([s[1:] for s in loads if s[0] == "x"], key=lambda part: (part[1] >= OPEN_TILES, part))
+
     with ExitStack() as ctx:
         sb = ctx.enter_context(tc.tile_pool(name="sb", bufs=1))
         ps = ctx.enter_context(tc.psum_pool(name="ps", bufs=1))
         ctx.enter_context(tc.manual_schedule())
 
-        prob_t = sb.tile([P, G, 16], BF16, name="prob_t")
-        negv = sb.tile([P, G, PACK], F32, name="negv")
-        alpha_t = sb.tile([P, PACK], BF16, name="alpha_t")
+        staged = sb.tile([P, N], BF16, name="staged")
+        columns = sb.tile([P, SLOTS, TURNED_COLUMNS], BF16, name="columns")
+        neg_variance = sb.tile([P, SLOTS, GROUPS], F32, name="neg_variance")
+        turned = ps.tile([P, SLOTS, P], BF16, name="turned", tag="bank6")
+        spread = ps.tile([P, SLOTS, P], BF16, name="spread", tag="bank7")
         alpha_all = sb.tile([P, N], F32, name="alpha_all")
-        ident = sb.tile([P, P], BF16, name="ident")
-        warm = sb.tile([P, 2], BF16, name="warm")
-        warm2 = sb.tile([P, 2], BF16, name="warm2")
-        c_plane = sb.tile([P, G, N], U8, name="c_plane", align_bytes=64)
-        d_plane = sb.tile([P, N], U8, name="d_plane", align_bytes=64)
-        c_t = [sb.tile([P, 2 * N], U8, name="c_t%d" % g, align_bytes=64) for g in range(G)]
-        d_t = [sb.tile([P, N], U32, name="d_t%d" % g, align_bytes=64) for g in range(G)]
-        e_raw = [sb.tile([P, PACK, N], BF16, name="e_raw%d" % g, align_bytes=64) for g in range(G)]
-        e_codes = [sb.tile([P, N], U32, name="e_codes%d" % g, align_bytes=64) for g in range(G)]
-        e_plane = [sb.tile([P, N], U8, name="e_plane%d" % g, align_bytes=64) for g in range(G)]
-        x_raw = {}
+        identity = sb.tile([P, P], BF16, name="identity")
+        first_in = sb.tile([P, 2], BF16, name="first_in")
+        first_out = sb.tile([P, 2], BF16, name="first_out")
+        c_plane = sb.tile([P, GROUPS, N], U8, name="c_plane", align_bytes=ALIGN)
+        d_plane = sb.tile([P, N], U8, name="d_plane", align_bytes=ALIGN)
+        c_codes = [sb.tile([P, 2 * N], U8, name="c_codes%d" % g, align_bytes=ALIGN) for g in range(GROUPS)]
+        d_codes = [sb.tile([P, N], U32, name="d_codes%d" % g, align_bytes=ALIGN) for g in range(GROUPS)]
+        e_rows = [sb.tile([P, SLOTS, N], BF16, name="e_rows%d" % g, align_bytes=ALIGN) for g in range(GROUPS)]
+        e_codes = [sb.tile([P, N], U32, name="e_codes%d" % g, align_bytes=ALIGN) for g in range(GROUPS)]
+        e_plane = [sb.tile([P, N], U8, name="e_plane%d" % g, align_bytes=ALIGN) for g in range(GROUPS)]
+        x_rows = {}
         a_rows = {}
-        for nm, g, c0, w in X_PIECES:
-            x_raw[nm] = sb.tile([P, PACK, w], BF16, name="xr_" + nm, align_bytes=64)
-            a_rows[nm] = sb.tile([P, PACK, w], BF16, name="ar_" + nm, align_bytes=64)
-        pieces = {nm: (g, c0, w) for nm, g, c0, w in X_PIECES}
-        grouped = {}
-        a_codes = {}
-        banks = {}
+        for part in x_parts:
+            shape = [P, SLOTS, P * part[2]]
+            x_rows[part] = sb.tile(shape, BF16, name="x_rows%d_%d_%d" % part, align_bytes=ALIGN)
+            a_rows[part] = sb.tile(shape, BF16, name="a_rows%d_%d_%d" % part, align_bytes=ALIGN)
+        zeros = sb.tile([P, SLOTS * P], BF16, name="zeros", align_bytes=ALIGN)
+        zero_codes = sb.tile([P, P], U32, name="zero_codes", align_bytes=ALIGN)
+        zero_plane = sb.tile([P, P], U8, name="zero_plane", align_bytes=ALIGN)
+        zero_sum = ps.tile([P, P], F32, name="zero_sum", tag="bank5")
+        laid = {}
+        a_operand = {}
+        sums = {}
         scaled = {}
-        result = {}
-        done = set()
 
-        def load(nm):
-            if nm == "prob":
-                nc.sync.dma_start(out=prob_t[:, :, 0:PACK], in_=prob.rearrange("(g p j) -> p g j", p=P, j=PACK))
-            elif nm[0] in "xy":
-                g, c0, w = pieces[nm]
-                src = x[512 * g : 512 * (g + 1), c0 : c0 + w].rearrange("(p j) w -> p j w", j=PACK)
-                nc.sync.dma_start(out=x_raw[nm][:], in_=src)
-            elif nm[0] == "e":
-                g = int(nm[1])
-                src = e[512 * g : 512 * (g + 1), :].rearrange("(p j) w -> p j w", j=PACK)
-                nc.sync.dma_start(out=e_raw[g][:], in_=src)
-            elif nm[:2] == "ds":
-                q = int(nm[2])
-                nc.sync.dma_start(
-                    out=d_plane[32 * q : 32 * q + 16, :].bitcast(I32),
-                    in_=d_scales[:, 4 * q : 4 * q + 4, :].bitcast(I32),
+        def idle_passes(count):
+            for i in range(count):
+                nc.tensor.matmul_mx(
+                    out=zero_sum[:], lhsT=zero_codes[:].bitcast(FP8X4), lhsT_scale=zero_plane[:],
+                    rhs=zero_codes[:].bitcast(FP8X4), rhs_scale=zero_plane[:], start=True, stop=True,
                 )
-            elif nm[:2] == "cs":
-                q = int(nm[2])
-                nc.sync.dma_start(
-                    out=c_plane[32 * q : 32 * q + 4, :, :].bitcast(I32),
-                    in_=c_scales[:, 4 * q : 4 * q + 4, :].rearrange("g r n -> r g n").bitcast(I32),
-                )
-            elif nm[0] == "d":
-                g = int(nm[1])
-                nc.sync.dma_start(
-                    out=d_t[g][:].bitcast(I32),
-                    in_=d_words[g].rearrange("p n t -> p (n t)").bitcast(I32),
-                )
+
+        def load(step):
+            what = step[0]
+            if what == "prob":
+                nc.sync.dma_start(out=staged[0:GROUPS, :], in_=prob.rearrange("(g k) -> g k", g=GROUPS))
+            elif what == "alpha":
+                nc.sync.dma_start(out=staged[GROUPS : GROUPS + 1, :], in_=alpha.rearrange("(o n) -> o n", o=1))
+            elif what == "x":
+                g, t, n = step[1:]
+                rows = x[K_PASS * g : K_PASS * (g + 1), P * t : P * (t + n)]
+                nc.sync.dma_start(out=x_rows[step[1:]][:], in_=rows.rearrange("(p j) w -> p j w", j=SLOTS))
+            elif what == "e":
+                rows = e[K_PASS * step[1] : K_PASS * (step[1] + 1), :]
+                nc.sync.dma_start(out=e_rows[step[1]][:], in_=rows.rearrange("(p j) w -> p j w", j=SLOTS))
+            elif what == "d_scales":
+                for q in range(QUADRANTS):
+                    nc.sync.dma_start(
+                        out=d_plane[32 * q : 32 * q + 4 * GROUPS, :].bitcast(I32),
+                        in_=d_scales[:, 4 * q : 4 * q + 4, :].bitcast(I32),
+                    )
+            elif what == "c_scales":
+                for q in range(QUADRANTS):
+                    nc.sync.dma_start(
+                        out=c_plane[32 * q : 32 * q + 4, :, :].bitcast(I32),
+                        in_=c_scales[:, 4 * q : 4 * q + 4, :].rearrange("g r n -> r g n").bitcast(I32),
+                    )
+            elif what == "d":
+                words = d_words[step[1]].rearrange("p n j -> p (n j)")
+                nc.sync.dma_start(out=d_codes[step[1]][:].bitcast(I32), in_=words.bitcast(I32))
             else:
-                g = int(nm[1])
-                nc.sync.dma_start(out=c_t[g][:].bitcast(I32), in_=c_words[g].bitcast(I32))
-            done.add(nm)
+                nc.sync.dma_start(out=c_codes[step[1]][:].bitcast(I32), in_=c_words[step[1]].bitcast(I32))
 
-        def interleave(on_vector, dst, src):
-            o = dst.rearrange("p (c i) t -> p c t i", i=4)
-            s = src.rearrange("p t (c i) -> p c t i", i=4)
-            if on_vector:
-                nc.vector.tensor_copy(out=o, in_=s)
-            else:
-                nc.scalar.copy(out=o, in_=s)
+        def covering(steps, g, t):
+            return [s for s in steps if s[-3] == g and s[-2] <= t < s[-2] + s[-1]][0]
 
-        def piece_of(g, c0):
-            for nm, pg, p0, w in X_PIECES:
-                if pg == g and p0 <= c0 < p0 + w:
-                    return nm, c0 - p0
-            raise ValueError(c0)
+        def quantise_step(operand, g, t):
+            return covering([s for s in on_vector if s[:2] == ("quantise", operand)], g, t)
 
-        def last_of(t, kinds):
-            return [s for s in PE_ORDER if s[0] in kinds and int(s[2]) == t][-1]
+        def sum_of(step):
+            return ("D" if step[1] == "D" else "CE", step[3])
 
-        def first_of(t, kinds):
-            return [s for s in PE_ORDER if s[0] in kinds and int(s[2]) == t][0]
+        def passes_into(key):
+            return [s for s in on_tensor if s[0] == "pass" and sum_of(s) == key]
 
-        def quant_step(kind, g, t):
-            for s in V_ORDER:
-                if s[:2] == "Q" + kind and int(s[2]) == g and int(s[3]) <= t < int(s[3]) + int(s[4]):
-                    return s
-            raise ValueError(t)
-
-        def needs(s):
-            k = s[:2]
-            if s == "nv":
-                return ["prob"]
-            if s == "alpha":
+        def needs(step):
+            what = step[0]
+            if what == "columns" or step[:2] == ("lay", "E"):
                 return []
-            if k == "SA":
-                return ["nv", s[2:]]
-            if k == "IA":
-                return ["SA" + piece_of(int(s[2]), 128 * int(s[3]))[0]]
-            if k == "IE":
-                return ["e" + s[2]]
-            if k in ("QA", "QE"):
-                g, t0, nt = int(s[2]), int(s[3]), int(s[4])
-                return [
-                    u for u in V_ORDER + S_ORDER
-                    if u[:2] == "I" + k[1] and int(u[2]) == g and t0 <= int(u[3]) < t0 + nt
-                ]
-            if k == "P1":
-                return [last_of(int(s[2]), "D"), "alpha"]
-            if k == "P2":
-                return [last_of(int(s[2]), "CE"), "P1" + s[2]]
-            g, t = int(s[1]), int(s[2])
-            d = [quant_step("A", g, t)]
-            if s[0] == "D":
-                d += ["d%d" % g, "ds3"] + (["P1%d" % (t - 4)] if t >= 4 else [])
-            else:
-                d += ["P2%d" % (t - 4)] if t >= 4 else ["alpha"]
-            if s[0] == "C":
-                d += ["c%d" % g, "cs3"]
-            if s[0] == "E":
-                d += [quant_step("E", g, u) for u in range(4)]
-            return d
+            if what in ("variance", "alpha"):
+                return [("columns",)]
+            if what == "weigh":
+                return [("variance",)]
+            if what == "lay":
+                return [("weigh",) + covering(x_parts, step[2], step[3])]
+            if what == "quantise":
+                first, runs = step[3:]
+                return [s for s in on_vector + on_scalar if s[:3] == ("lay",) + step[1:3] and first <= s[3] < first + runs]
+            if what == "scale":
+                return [passes_into(("D", step[1]))[-1], ("alpha",)]
+            if what == "add":
+                return [passes_into(("CE", step[1]))[-1], ("scale", step[1])]
+            if what == "add_c_last":
+                return [passes_into(("CE", LAST))[-1], ("scale", LAST)]
+            if what == "add_e_last":
+                return [("half_pass", step[1], GROUPS - 1), ("add_c_last",)]
+            if what == "half_pass":
+                return [("add", OPEN_TILES), ("add", OPEN_TILES + 1)]
+            moving, g, t = step[1:]
+            earlier = [quantise_step("A", g, t), ("columns",)]
+            if moving == "E":
+                earlier += [quantise_step("E", g, 0)]
+            if t >= OPEN_TILES:
+                earlier += [("scale" if moving == "D" else "add", t - OPEN_TILES)]
+            elif t == OPEN_TILES - 1 and moving != "D":
+                earlier += [("alpha",)]
+            return earlier
 
-        def group_tile(kind, g, t):
-            q = quant_step(kind, g, t)
-            if q not in grouped:
-                grouped[q] = sb.tile([P, 128 * int(q[4]), PACK], BF16, name="gr_" + q, align_bytes=64)
-            return grouped[q], 128 * (t - int(q[3]))
-
-        def step(s, on_vector):
-            k = s[:2]
-            if s == "nv":
+        def emit(step):
+            what = step[0]
+            if what == "columns":
+                by_slot = staged[:].rearrange("r (p j) -> r j p", j=SLOTS)
+                for j in range(SLOTS):
+                    nc.tensor.transpose(turned[:, j, :], by_slot[:, j, :], identity[:])
+                nc.scalar.copy(out=columns[:], in_=turned[:, :, 0:TURNED_COLUMNS])
+                idle_passes(IDLE_PASSES[1])
+                for j in range(SLOTS):
+                    repeated = columns[:, j, GROUPS : GROUPS + 1].to_broadcast([P, P])
+                    nc.tensor.transpose(spread[:, j, :], repeated, identity[:])
+                idle_passes(IDLE_PASSES[2])
+            elif what == "alpha":
+                nc.scalar.copy(
+                    out=alpha_all[:].rearrange("q (p j) -> q p j", j=SLOTS),
+                    in_=spread[:].rearrange("q j p -> q p j"),
+                )
+            elif what == "variance":
                 nc.vector.scalar_tensor_tensor(
-                    out=negv[:], in0=prob_t[:, :, 0:PACK], scalar=1.0, in1=prob_t[:, :, 0:PACK],
+                    out=neg_variance[:], in0=columns[:, :, 0:GROUPS], scalar=1.0, in1=columns[:, :, 0:GROUPS],
                     op0=ALU.subtract, op1=ALU.mult,
                 )
-            elif s == "alpha":
-                spread = ps.tile([P, PACK, P], BF16, name="spread", tag="bank7")
-                for m in range(PACK):
-                    nc.tensor.transpose(spread[:, m, :], alpha_t[:, m : m + 1].to_broadcast([P, P]), ident[:])
-                nc.scalar.copy(
-                    out=alpha_all[:].rearrange("q (p m) -> q p m", m=PACK),
-                    in_=spread[:].rearrange("q m p -> q p m"),
-                )
-            elif k == "SA":
-                nm = s[2:]
-                g = pieces[nm][0]
-                for j in range(PACK):
+            elif what == "weigh":
+                g = step[1]
+                for j in range(SLOTS):
                     nc.vector.tensor_scalar(
-                        out=a_rows[nm][:, j, :], in0=x_raw[nm][:, j, :], scalar1=negv[:, g, j : j + 1],
-                        scalar2=-1.0, op0=ALU.mult, op1=ALU.mult,
+                        out=a_rows[step[1:]][:, j, :], in0=x_rows[step[1:]][:, j, :],
+                        scalar1=neg_variance[:, j, g : g + 1], scalar2=-1.0, op0=ALU.mult, op1=ALU.mult,
                     )
-            elif k in ("IA", "IE"):
-                g, t0, nt = int(s[2]), int(s[3]), int(s[4])
-                dst, o0 = group_tile(k[1], g, t0)
-                if k == "IA":
-                    nm, c0 = piece_of(g, 128 * t0)
-                    src = a_rows[nm][:, :, c0 : c0 + 128 * nt]
+            elif what == "lay":
+                operand, g, first, runs = step[1:]
+                target = quantise_step(operand, g, first)
+                if target not in laid:
+                    name = "laid_%s%d_%d" % target[1:4]
+                    laid[target] = sb.tile([P, P * target[4], SLOTS], BF16, name=name, align_bytes=ALIGN)
+                at = P * (first - target[3])
+                if operand == "A":
+                    part = covering(x_parts, g, first)
+                    source = a_rows[part][:, :, P * (first - part[1]) : P * (first - part[1] + runs)]
                 else:
-                    src = e_raw[g][:, :, 128 * t0 : 128 * (t0 + nt)]
-                interleave(on_vector, dst[:, o0 : o0 + 128 * nt, :], src)
-            elif k == "QA":
-                g, t0, nt = int(s[2]), int(s[3]), int(s[4])
-                codes = sb.tile([P, 128 * nt], U32, name="ac_" + s, align_bytes=64)
-                plane = sb.tile([P, 128 * nt], U8, name="ap_" + s, align_bytes=64)
-                nc.vector.quantize_mx(
-                    out=codes[:].bitcast(FP8X4), scales=plane[:],
-                    in_=grouped[s][:].rearrange("p w j -> p (w j)"),
-                )
-                for u in range(nt):
-                    a_codes[(g, t0 + u)] = (codes[:, 128 * u : 128 * (u + 1)], plane[:, 128 * u : 128 * (u + 1)])
-            elif k == "QE":
-                g, t0, nt = int(s[2]), int(s[3]), int(s[4])
-                cols = slice(128 * t0, 128 * (t0 + nt))
-                nc.vector.quantize_mx(
-                    out=e_codes[g][:, cols].bitcast(FP8X4), scales=e_plane[g][:, cols],
-                    in_=grouped[s][:].rearrange("p w j -> p (w j)"),
-                )
-            elif k == "P1":
-                t = int(s[2])
-                scaled[t] = sb.tile([P, N], F32, name="scaled%d" % t)
-                nc.vector.tensor_tensor(out=scaled[t][:], in0=banks[("D", t)][:], in1=alpha_all[:], op=ALU.mult)
-            elif k == "P2":
-                t = int(s[2])
-                result[t] = sb.tile([P, N], F32, name="result%d" % t)
-                parts = 2 if t == 7 else 1
-                w = N // parts
-                for h in range(parts):
-                    cols = slice(h * w, (h + 1) * w)
-                    nc.vector.tensor_tensor(
-                        out=result[t][:, cols], in0=banks[("P", t)][:, cols], in1=scaled[t][:, cols], op=ALU.add
-                    )
-                    nc.sync.dma_start(out=out[128 * t : 128 * (t + 1), cols], in_=result[t][:, cols])
-            else:
-                g, t = int(s[1]), int(s[2])
-                kinds = "D" if s[0] == "D" else "CE"
-                key = ("D" if s[0] == "D" else "P", t)
-                if key not in banks:
-                    b = t % 4 + (0 if s[0] == "D" else 4)
-                    banks[key] = ps.tile([P, N], F32, name="acc%s%d" % key, tag="bank%d" % b)
-                codes, plane = a_codes[(g, t)]
-                if s[0] == "D":
-                    rhs, rs = d_t[g][:].bitcast(FP8X4), d_plane[4 * g :, :]
-                elif s[0] == "C":
-                    rhs, rs = c_t[g][:].bitcast(FP4X4), c_plane[:, g, :]
+                    source = e_rows[g][:, :, P * first : P * (first + runs)]
+                dst = laid[target][:, at : at + P * runs, :].rearrange("p (c i) j -> p c j i", i=4)
+                src = source.rearrange("p j (c i) -> p c j i", i=4)
+                if step in on_vector:
+                    nc.vector.tensor_copy(out=dst, in_=src)
                 else:
-                    rhs, rs = e_codes[g][:].bitcast(FP8X4), e_plane[g][:]
+                    nc.scalar.copy(out=dst, in_=src)
+            elif what == "quantise":
+                operand, g, first, runs = step[1:]
+                if operand == "A":
+                    codes = sb.tile([P, P * runs], U32, name="a_codes%d_%d" % (g, first), align_bytes=ALIGN)
+                    plane = sb.tile([P, P * runs], U8, name="a_plane%d_%d" % (g, first), align_bytes=ALIGN)
+                    for u in range(runs):
+                        a_operand[(g, first + u)] = (codes[:, P * u : P * (u + 1)], plane[:, P * u : P * (u + 1)])
+                else:
+                    codes, plane = e_codes[g], e_plane[g]
+                nc.vector.quantize_mx(
+                    out=codes[:].bitcast(FP8X4), scales=plane[:], in_=laid[step][:].rearrange("p w j -> p (w j)")
+                )
+            elif what == "pass":
+                moving, g, t = step[1:]
+                key = sum_of(step)
+                if key not in sums:
+                    bank = t % OPEN_TILES + (0 if moving == "D" else OPEN_TILES)
+                    sums[key] = ps.tile([P, N], F32, name="sum_%s%d" % key, tag="bank%d" % bank)
+                if moving == "D":
+                    rhs, rhs_plane = d_codes[g][:].bitcast(FP8X4), d_plane[4 * g :, :]
+                elif moving == "C":
+                    rhs, rhs_plane = c_codes[g][:].bitcast(FP4X4), c_plane[:, g, :]
+                else:
+                    rhs, rhs_plane = e_codes[g][:].bitcast(FP8X4), e_plane[g][:]
+                codes, plane = a_operand[(g, t)]
                 nc.tensor.matmul_mx(
-                    out=banks[key][:], lhsT=codes.bitcast(FP8X4), lhsT_scale=plane, rhs=rhs, rhs_scale=rs,
-                    start=(s == first_of(t, kinds)), stop=(s == last_of(t, kinds)),
+                    out=sums[key][:], lhsT=codes.bitcast(FP8X4), lhsT_scale=plane, rhs=rhs, rhs_scale=rhs_plane,
+                    start=(step == passes_into(key)[0]), stop=(step == passes_into(key)[-1]),
                 )
-            done.add(s)
+            elif what == "half_pass":
+                h, g = step[1:]
+                cols = slice(HALF * h, HALF * (h + 1))
+                if g == 0:
+                    bank = "bank%d" % (OPEN_TILES + h)
+                    sums[("half", h)] = ps.tile([P, HALF], F32, name="sum_half%d" % h, tag=bank)
+                codes, plane = a_operand[(g, LAST)]
+                nc.tensor.matmul_mx(
+                    out=sums[("half", h)][:], lhsT=codes.bitcast(FP8X4), lhsT_scale=plane,
+                    rhs=e_codes[g][:, cols].bitcast(FP8X4), rhs_scale=e_plane[g][:, cols],
+                    start=(g == 0), stop=(g == GROUPS - 1),
+                )
+            elif what == "scale":
+                t = step[1]
+                scaled[t] = sb.tile([P, N], F32, name="scaled%d" % t)
+                nc.vector.tensor_tensor(out=scaled[t][:], in0=sums[("D", t)][:], in1=alpha_all[:], op=ALU.mult)
+            elif what == "add":
+                t = step[1]
+                result = sb.tile([P, N], F32, name="result%d" % t)
+                nc.vector.tensor_tensor(out=result[:], in0=sums[("CE", t)][:], in1=scaled[t][:], op=ALU.add)
+                nc.sync.dma_start(out=out[P * t : P * (t + 1), :], in_=result[:])
+            elif what == "add_c_last":
+                scaled["last"] = sb.tile([P, N], F32, name="scaled_last")
+                nc.vector.tensor_tensor(
+                    out=scaled["last"][:], in0=sums[("CE", LAST)][:], in1=scaled[LAST][:], op=ALU.add
+                )
+            else:
+                h = step[1]
+                cols = slice(HALF * h, HALF * (h + 1))
+                result = sb.tile([P, HALF], F32, name="result_half%d" % h)
+                nc.vector.tensor_tensor(out=result[:], in0=sums[("half", h)][:], in1=scaled["last"][:, cols], op=ALU.add)
+                nc.sync.dma_start(out=out[P * LAST :, cols], in_=result[:])
 
-        nc.gpsimd.dma_start(out=alpha_t[:], in_=alpha.rearrange("(p m) -> p m", m=PACK))
-        make_identity(nc, ident[:])
+        nc.gpsimd.memset(staged[:].bitcast(I32), 0)
+        make_identity(nc, identity[:])
         nc.vector.memset(d_plane[:].bitcast(I32), 0)
+        nc.vector.memset(zeros[:], 0.0)
+        nc.vector.memset(first_in[:], 0.0)
+        nc.vector.quantize_mx(out=zero_codes[:].bitcast(FP8X4), scales=zero_plane[:], in_=zeros[:])
+        idle_passes(IDLE_PASSES[0])
         nc.vector.memset(c_plane[:].rearrange("p g n -> p (g n)").bitcast(I32), 0)
-        nc.vector.memset(warm[:], 0.0)
-        nc.scalar.copy(out=warm2[:], in_=warm[:])
-        for nm in LOADS:
-            load(nm)
-        queues = [(list(V_ORDER), True), (list(S_ORDER), False), (list(PE_ORDER), False)]
-        while any(q for q, v in queues):
-            moved = False
-            for q, v in queues:
-                while q and all(d in done for d in needs(q[0])):
-                    step(q[0], v)
-                    q.remove(q[0])
-                    moved = True
-            assert moved
+        nc.scalar.copy(out=first_out[:], in_=first_in[:])
+        for step in loads:
+            load(step)
+
+        waiting = [list(on_vector), list(on_scalar), list(on_tensor)]
+        written = set()
+        while any(waiting):
+            for steps in waiting:
+                while steps and all(s in written for s in needs(steps[0])):
+                    emit(steps[0])
+                    written.add(steps[0])
+                    steps.remove(steps[0])

from contextlib import ExitStack

import concourse.mybir as mybir
from concourse.masks import make_identity

M, F, N = 2048, 1024, 512
FLOPS = 3 * 2 * M * F * N

F32 = mybir.dt.float32
BF16 = mybir.dt.bfloat16
I32 = mybir.dt.int32
U32 = mybir.dt.uint32
U8 = mybir.dt.uint8
FP8X4 = mybir.dt.float8_e4m3fn_x4
FP4X4 = mybir.dt.float4_e2m1fn_x4
ALU = mybir.AluOpType

P = 128
SLOTS = 4
K_PASS = P * SLOTS
GROUPS = M // K_PASS
TILES = F // P
OPEN_TILES = 4
LAST = TILES - 1
HALF = N // 2
QUADRANTS = 4
ALIGN = 256
TURNED_COLUMNS = 8
IDLE_PASSES = (10, 3, 10)

LOAD_ORDER = [
    "alpha", "prob", "x 0 0 4", "d_scales", "d 0", "e 0", "x 1 0 4", "c 0", "c_scales", "x 2 0 4", "e 1",
    "d 1", "c 1", "x 3 0 4", "c 2", "d 2", "e 2", "e 3", "d 3", "x 0 4 2", "c 3", "x 1 4 4", "x 2 4 4",
    "x 0 6 2", "x 3 4 4",
]

VECTOR_ORDER = [
    "variance", "weigh 0 0 4", "lay A 0 0 1", "lay A 0 1 1", "quantise A 0 0 1", "quantise A 0 2 1",
    "quantise A 0 1 1", "lay E 0 2 2", "quantise A 0 3 1", "weigh 1 0 4", "quantise E 0 0 4", "lay A 1 2 1",
    "weigh 2 0 4", "quantise A 1 2 2", "quantise A 1 0 2", "lay E 1 2 2", "lay A 2 0 1", "quantise E 1 0 4",
    "weigh 3 0 4", "quantise A 2 0 2", "lay A 3 2 1", "lay A 3 1 1", "quantise A 2 2 2", "lay E 2 2 2",
    "quantise A 3 2 2", "quantise A 3 0 2", "lay E 3 2 2", "quantise E 2 0 4", "weigh 0 4 2", "scale 1",
    "quantise E 3 0 4", "weigh 1 4 4", "scale 0", "quantise A 0 4 2", "add 0", "add 1", "weigh 2 4 4",
    "quantise A 1 4 2", "weigh 0 6 2", "weigh 3 4 4", "quantise A 2 4 2", "lay A 3 4 2", "scale 2",
    "quantise A 3 4 2", "lay A 1 6 2", "quantise A 0 6 2", "quantise A 1 6 2", "add 2", "quantise A 2 6 2",
    "quantise A 3 6 2", "scale 5", "scale 3", "scale 4", "add 3", "scale 6", "add 4", "add 6", "add 5",
    "scale 7", "add_c_last", "add_e_last 0", "add_e_last 1",
]
SCALAR_ORDER = [
    "columns", "alpha", "lay A 0 2 1", "lay A 0 3 1", "lay E 0 0 2", "lay A 1 0 1", "lay A 1 3 1",
    "lay A 1 1 1", "lay E 1 0 2", "lay A 2 1 1", "lay A 2 3 1", "lay A 2 2 1", "lay A 3 0 1", "lay A 3 3 1",
    "lay E 2 0 2", "lay E 3 0 2", "lay A 0 5 1", "lay A 0 4 1", "lay A 1 4 2", "lay A 2 4 2", "lay A 0 6 2",
    "lay A 2 6 2", "lay A 3 6 2",
]
FIRST_SWEEP = ["D0", "C0", "E0", "D1", "C1", "E1", "D2", "C2", "D3", "E2"]


def tensor_order():
    order = ["pass %s %s %d" % (b[0], b[1], t) for b in FIRST_SWEEP for t in range(OPEN_TILES)]
    order += ["pass %s %d %d" % (w, GROUPS - 1, t) for t in range(OPEN_TILES) for w in "CE"]
    for g in range(GROUPS):
        order += ["pass %s %d %d" % (w, g, t) for w in ("DCE" if g == 0 else "DEC") for t in (4, 5)]
    order += ["pass %s %d %d" % (w, g, LAST - 1) for w in "DCE" for g in range(GROUPS)]
    order += ["pass %s %d %d" % (w, g, LAST) for w in "DC" for g in range(GROUPS)]
    order += ["half_pass %d %d" % (h, g) for h in range(2) for g in range(GROUPS)]
    return order


def parse(step):
    return tuple(w if w[0] not in "0123456789" else int(w) for w in step.split())


def tile_logistic_hessian_block_s10_kernel(
    tc, x, prob, c_words, c_scales, d_words, d_scales, e, alpha, out
):
    nc = tc.nc
    loads = [parse(s) for s in LOAD_ORDER]
    on_vector = [parse(s) for s in VECTOR_ORDER]
    on_scalar = [parse(s) for s in SCALAR_ORDER]
    on_tensor = [parse(s) for s in tensor_order()]
    x_parts = sorted([s[1:] for s in loads if s[0] == "x"], key=lambda part: (part[1] >= OPEN_TILES, part))

    with ExitStack() as ctx:
        sb = ctx.enter_context(tc.tile_pool(name="sb", bufs=1))
        ps = ctx.enter_context(tc.psum_pool(name="ps", bufs=1))
        ctx.enter_context(tc.manual_schedule())

        staged = sb.tile([P, N], BF16, name="staged")
        columns = sb.tile([P, SLOTS, TURNED_COLUMNS], BF16, name="columns")
        neg_variance = sb.tile([P, SLOTS, GROUPS], F32, name="neg_variance")
        turned = ps.tile([P, SLOTS, P], BF16, name="turned", tag="bank6")
        spread = ps.tile([P, SLOTS, P], BF16, name="spread", tag="bank7")
        alpha_all = sb.tile([P, N], F32, name="alpha_all")
        identity = sb.tile([P, P], BF16, name="identity")
        first_in = sb.tile([P, 2], BF16, name="first_in")
        first_out = sb.tile([P, 2], BF16, name="first_out")
        c_plane = sb.tile([P, GROUPS, N], U8, name="c_plane", align_bytes=ALIGN)
        d_plane = sb.tile([P, N], U8, name="d_plane", align_bytes=ALIGN)
        c_codes = [sb.tile([P, 2 * N], U8, name="c_codes%d" % g, align_bytes=ALIGN) for g in range(GROUPS)]
        d_codes = [sb.tile([P, N], U32, name="d_codes%d" % g, align_bytes=ALIGN) for g in range(GROUPS)]
        e_rows = [sb.tile([P, SLOTS, N], BF16, name="e_rows%d" % g, align_bytes=ALIGN) for g in range(GROUPS)]
        e_codes = [sb.tile([P, N], U32, name="e_codes%d" % g, align_bytes=ALIGN) for g in range(GROUPS)]
        e_plane = [sb.tile([P, N], U8, name="e_plane%d" % g, align_bytes=ALIGN) for g in range(GROUPS)]
        x_rows = {}
        a_rows = {}
        for part in x_parts:
            shape = [P, SLOTS, P * part[2]]
            x_rows[part] = sb.tile(shape, BF16, name="x_rows%d_%d_%d" % part, align_bytes=ALIGN)
            a_rows[part] = sb.tile(shape, BF16, name="a_rows%d_%d_%d" % part, align_bytes=ALIGN)
        zeros = sb.tile([P, SLOTS * P], BF16, name="zeros", align_bytes=ALIGN)
        zero_codes = sb.tile([P, P], U32, name="zero_codes", align_bytes=ALIGN)
        zero_plane = sb.tile([P, P], U8, name="zero_plane", align_bytes=ALIGN)
        zero_sum = ps.tile([P, P], F32, name="zero_sum", tag="bank5")
        laid = {}
        a_operand = {}
        sums = {}
        scaled = {}

        def idle_passes(count):
            for i in range(count):
                nc.tensor.matmul_mx(
                    out=zero_sum[:], lhsT=zero_codes[:].bitcast(FP8X4), lhsT_scale=zero_plane[:],
                    rhs=zero_codes[:].bitcast(FP8X4), rhs_scale=zero_plane[:], start=True, stop=True,
                )

        def load(step):
            what = step[0]
            if what == "prob":
                nc.sync.dma_start(out=staged[0:GROUPS, :], in_=prob.rearrange("(g k) -> g k", g=GROUPS))
            elif what == "alpha":
                nc.sync.dma_start(out=staged[GROUPS : GROUPS + 1, :], in_=alpha.rearrange("(o n) -> o n", o=1))
            elif what == "x":
                g, t, n = step[1:]
                rows = x[K_PASS * g : K_PASS * (g + 1), P * t : P * (t + n)]
                nc.sync.dma_start(out=x_rows[step[1:]][:], in_=rows.rearrange("(p j) w -> p j w", j=SLOTS))
            elif what == "e":
                rows = e[K_PASS * step[1] : K_PASS * (step[1] + 1), :]
                nc.sync.dma_start(out=e_rows[step[1]][:], in_=rows.rearrange("(p j) w -> p j w", j=SLOTS))
            elif what == "d_scales":
                for q in range(QUADRANTS):
                    nc.sync.dma_start(
                        out=d_plane[32 * q : 32 * q + 4 * GROUPS, :].bitcast(I32),
                        in_=d_scales[:, 4 * q : 4 * q + 4, :].bitcast(I32),
                    )
            elif what == "c_scales":
                for q in range(QUADRANTS):
                    nc.sync.dma_start(
                        out=c_plane[32 * q : 32 * q + 4, :, :].bitcast(I32),
                        in_=c_scales[:, 4 * q : 4 * q + 4, :].rearrange("g r n -> r g n").bitcast(I32),
                    )
            elif what == "d":
                words = d_words[step[1]].rearrange("p n j -> p (n j)")
                nc.sync.dma_start(out=d_codes[step[1]][:].bitcast(I32), in_=words.bitcast(I32))
            else:
                nc.sync.dma_start(out=c_codes[step[1]][:].bitcast(I32), in_=c_words[step[1]].bitcast(I32))

        def covering(steps, g, t):
            return [s for s in steps if s[-3] == g and s[-2] <= t < s[-2] + s[-1]][0]

        def quantise_step(operand, g, t):
            return covering([s for s in on_vector if s[:2] == ("quantise", operand)], g, t)

        def sum_of(step):
            return ("D" if step[1] == "D" else "CE", step[3])

        def passes_into(key):
            return [s for s in on_tensor if s[0] == "pass" and sum_of(s) == key]

        def needs(step):
            what = step[0]
            if what == "columns" or step[:2] == ("lay", "E"):
                return []
            if what in ("variance", "alpha"):
                return [("columns",)]
            if what == "weigh":
                return [("variance",)]
            if what == "lay":
                return [("weigh",) + covering(x_parts, step[2], step[3])]
            if what == "quantise":
                first, runs = step[3:]
                return [s for s in on_vector + on_scalar if s[:3] == ("lay",) + step[1:3] and first <= s[3] < first + runs]
            if what == "scale":
                return [passes_into(("D", step[1]))[-1], ("alpha",)]
            if what == "add":
                return [passes_into(("CE", step[1]))[-1], ("scale", step[1])]
            if what == "add_c_last":
                return [passes_into(("CE", LAST))[-1], ("scale", LAST)]
            if what == "add_e_last":
                return [("half_pass", step[1], GROUPS - 1), ("add_c_last",)]
            if what == "half_pass":
                return [("add", OPEN_TILES), ("add", OPEN_TILES + 1)]
            moving, g, t = step[1:]
            earlier = [quantise_step("A", g, t), ("columns",)]
            if moving == "E":
                earlier += [quantise_step("E", g, 0)]
            if t >= OPEN_TILES:
                earlier += [("scale" if moving == "D" else "add", t - OPEN_TILES)]
            elif t == OPEN_TILES - 1 and moving != "D":
                earlier += [("alpha",)]
            return earlier

        def emit(step):
            what = step[0]
            if what == "columns":
                by_slot = staged[:].rearrange("r (p j) -> r j p", j=SLOTS)
                for j in range(SLOTS):
                    nc.tensor.transpose(turned[:, j, :], by_slot[:, j, :], identity[:])
                nc.scalar.copy(out=columns[:], in_=turned[:, :, 0:TURNED_COLUMNS])
                idle_passes(IDLE_PASSES[1])
                for j in range(SLOTS):
                    repeated = columns[:, j, GROUPS : GROUPS + 1].to_broadcast([P, P])
                    nc.tensor.transpose(spread[:, j, :], repeated, identity[:])
                idle_passes(IDLE_PASSES[2])
            elif what == "alpha":
                nc.scalar.copy(
                    out=alpha_all[:].rearrange("q (p j) -> q p j", j=SLOTS),
                    in_=spread[:].rearrange("q j p -> q p j"),
                )
            elif what == "variance":
                nc.vector.scalar_tensor_tensor(
                    out=neg_variance[:], in0=columns[:, :, 0:GROUPS], scalar=1.0, in1=columns[:, :, 0:GROUPS],
                    op0=ALU.subtract, op1=ALU.mult,
                )
            elif what == "weigh":
                g = step[1]
                for j in range(SLOTS):
                    nc.vector.tensor_scalar(
                        out=a_rows[step[1:]][:, j, :], in0=x_rows[step[1:]][:, j, :],
                        scalar1=neg_variance[:, j, g : g + 1], scalar2=-1.0, op0=ALU.mult, op1=ALU.mult,
                    )
            elif what == "lay":
                operand, g, first, runs = step[1:]
                target = quantise_step(operand, g, first)
                if target not in laid:
                    name = "laid_%s%d_%d" % target[1:4]
                    laid[target] = sb.tile([P, P * target[4], SLOTS], BF16, name=name, align_bytes=ALIGN)
                at = P * (first - target[3])
                if operand == "A":
                    part = covering(x_parts, g, first)
                    source = a_rows[part][:, :, P * (first - part[1]) : P * (first - part[1] + runs)]
                else:
                    source = e_rows[g][:, :, P * first : P * (first + runs)]
                dst = laid[target][:, at : at + P * runs, :].rearrange("p (c i) j -> p c j i", i=4)
                src = source.rearrange("p j (c i) -> p c j i", i=4)
                if step in on_vector:
                    nc.vector.tensor_copy(out=dst, in_=src)
                else:
                    nc.scalar.copy(out=dst, in_=src)
            elif what == "quantise":
                operand, g, first, runs = step[1:]
                if operand == "A":
                    codes = sb.tile([P, P * runs], U32, name="a_codes%d_%d" % (g, first), align_bytes=ALIGN)
                    plane = sb.tile([P, P * runs], U8, name="a_plane%d_%d" % (g, first), align_bytes=ALIGN)
                    for u in range(runs):
                        a_operand[(g, first + u)] = (codes[:, P * u : P * (u + 1)], plane[:, P * u : P * (u + 1)])
                else:
                    codes, plane = e_codes[g], e_plane[g]
                nc.vector.quantize_mx(
                    out=codes[:].bitcast(FP8X4), scales=plane[:], in_=laid[step][:].rearrange("p w j -> p (w j)")
                )
            elif what == "pass":
                moving, g, t = step[1:]
                key = sum_of(step)
                if key not in sums:
                    bank = t % OPEN_TILES + (0 if moving == "D" else OPEN_TILES)
                    sums[key] = ps.tile([P, N], F32, name="sum_%s%d" % key, tag="bank%d" % bank)
                if moving == "D":
                    rhs, rhs_plane = d_codes[g][:].bitcast(FP8X4), d_plane[4 * g :, :]
                elif moving == "C":
                    rhs, rhs_plane = c_codes[g][:].bitcast(FP4X4), c_plane[:, g, :]
                else:
                    rhs, rhs_plane = e_codes[g][:].bitcast(FP8X4), e_plane[g][:]
                codes, plane = a_operand[(g, t)]
                nc.tensor.matmul_mx(
                    out=sums[key][:], lhsT=codes.bitcast(FP8X4), lhsT_scale=plane, rhs=rhs, rhs_scale=rhs_plane,
                    start=(step == passes_into(key)[0]), stop=(step == passes_into(key)[-1]),
                )
            elif what == "half_pass":
                h, g = step[1:]
                cols = slice(HALF * h, HALF * (h + 1))
                if g == 0:
                    bank = "bank%d" % (OPEN_TILES + h)
                    sums[("half", h)] = ps.tile([P, HALF], F32, name="sum_half%d" % h, tag=bank)
                codes, plane = a_operand[(g, LAST)]
                nc.tensor.matmul_mx(
                    out=sums[("half", h)][:], lhsT=codes.bitcast(FP8X4), lhsT_scale=plane,
                    rhs=e_codes[g][:, cols].bitcast(FP8X4), rhs_scale=e_plane[g][:, cols],
                    start=(g == 0), stop=(g == GROUPS - 1),
                )
            elif what == "scale":
                t = step[1]
                scaled[t] = sb.tile([P, N], F32, name="scaled%d" % t)
                nc.vector.tensor_tensor(out=scaled[t][:], in0=sums[("D", t)][:], in1=alpha_all[:], op=ALU.mult)
            elif what == "add":
                t = step[1]
                result = sb.tile([P, N], F32, name="result%d" % t)
                nc.vector.tensor_tensor(out=result[:], in0=sums[("CE", t)][:], in1=scaled[t][:], op=ALU.add)
                nc.sync.dma_start(out=out[P * t : P * (t + 1), :], in_=result[:])
            elif what == "add_c_last":
                scaled["last"] = sb.tile([P, N], F32, name="scaled_last")
                nc.vector.tensor_tensor(
                    out=scaled["last"][:], in0=sums[("CE", LAST)][:], in1=scaled[LAST][:], op=ALU.add
                )
            else:
                h = step[1]
                cols = slice(HALF * h, HALF * (h + 1))
                result = sb.tile([P, HALF], F32, name="result_half%d" % h)
                nc.vector.tensor_tensor(out=result[:], in0=sums[("half", h)][:], in1=scaled["last"][:, cols], op=ALU.add)
                nc.sync.dma_start(out=out[P * LAST :, cols], in_=result[:])

        nc.gpsimd.memset(staged[:].bitcast(I32), 0)
        make_identity(nc, identity[:])
        nc.vector.memset(d_plane[:].bitcast(I32), 0)
        nc.vector.memset(zeros[:], 0.0)
        nc.vector.memset(first_in[:], 0.0)
        nc.vector.quantize_mx(out=zero_codes[:].bitcast(FP8X4), scales=zero_plane[:], in_=zeros[:])
        idle_passes(IDLE_PASSES[0])
        nc.vector.memset(c_plane[:].rearrange("p g n -> p (g n)").bitcast(I32), 0)
        nc.scalar.copy(out=first_out[:], in_=first_in[:])
        for step in loads:
            load(step)

        waiting = [list(on_vector), list(on_scalar), list(on_tensor)]
        written = set()
        while any(waiting):
            for steps in waiting:
                while steps and all(s in written for s in needs(steps[0])):
                    emit(steps[0])
                    written.add(steps[0])
                    steps.remove(steps[0])
